import numpy as np
import ml_dtypes


def mxq(x, axis, fmt="e4m3"):
    dtype, down = {"e4m3": (ml_dtypes.float8_e4m3fn, 7), "e5m2": (ml_dtypes.float8_e5m2, 14)}[fmt]
    v = np.moveaxis(np.asarray(x, np.float32).astype(ml_dtypes.bfloat16).astype(np.float64), axis, -1)
    blocks = v.reshape(v.shape[:-1] + (-1, 32))
    amax = np.abs(blocks).max(-1, keepdims=True)
    byte = np.maximum(np.where(amax > 0, np.frexp(amax)[1] - 1 + 127, 0) - down, 1)
    scale = np.exp2(byte - 127.0)
    codes = (blocks / scale).astype(np.float32).astype(dtype).astype(np.float64)
    return np.moveaxis((codes * scale).reshape(v.shape), -1, axis)


WIDE = False


def mx_kscale(k):
    if not WIDE:
        return np.ones(k)
    levels = np.array([10, -10, 5, -5, 0])
    if k % 512:
        return np.exp2(np.random.permutation(np.resize(levels, k // 32))).repeat(32)
    a = np.empty((k // 512, 16))
    for p in range(k // 512):
        a[p, :8] = np.random.permutation(np.resize(levels, 8))
        for g in range(8):
            far = levels[np.abs(levels - a[p, g]) >= 10]
            a[p, g + 8] = far[np.random.randint(len(far))]
    return np.exp2(a.ravel()).repeat(32)


def f64(x):
    return np.asarray(x).astype(np.float64)


def striped(idx):
    return np.tile(idx.reshape(-1, 16).T, (8, 1)).astype(np.uint16)


def unstriped(offs):
    return offs[:16].T.reshape(-1).astype(np.int64)


def striped8(idx):
    return np.concatenate([x.reshape(-1, 16).T for x in idx]).astype(np.uint16)


def runs(offs, k):
    lists = np.stack([offs[16 * r : 16 * r + 16].T.reshape(-1) for r in range(8)]).astype(np.int64)
    return lists[np.arange(k) % 512 // 64]


def pack_weight(w):
    k, n = w.shape
    w = f64(np.asarray(w, np.float32).astype(ml_dtypes.bfloat16)).reshape(k // 32, 32, n)
    amax = np.abs(w).max(1)
    byte = np.clip(np.where(amax > 0, np.frexp(amax)[1] - 1 + 127 - 7, 1), 1, 254)
    scaled = (w * np.exp2(127.0 - byte)[:, None, :]).reshape(k, n).astype(np.float32)
    words = np.ascontiguousarray(scaled.reshape(k // 512, 128, 4, n).transpose(0, 1, 3, 2)).astype(ml_dtypes.float8_e4m3fn).view(np.uint8)
    return words, np.ascontiguousarray(byte.astype(np.uint8).reshape(k // 512, 16, n))


def unpack_weight(words, scales):
    g, p, n, _ = words.shape
    vals = np.ascontiguousarray(words).view(ml_dtypes.float8_e4m3fn).astype(np.float64) * np.repeat(np.exp2(scales.astype(np.float64) - 127.0), 8, axis=1)[..., None]
    return vals.transpose(0, 1, 3, 2).reshape(g * 512, n)


def sigmoid(v):
    return 1.0 / (1.0 + np.exp(-np.maximum(v, -700.0)))

def planes(y):
    n, m = y.shape
    v = y.astype(np.float32).astype(ml_dtypes.bfloat16).astype(np.float64).reshape(n // 32, 32, m)
    top = np.abs(v).max(1)
    byte = np.clip(np.where(top > 0, np.frexp(top)[1] - 1 + 127 - 7, 1), 1, 254)
    codes = (v * np.exp2(127.0 - byte)[:, None, :]).reshape(n, m).astype(np.float32).astype(ml_dtypes.float8_e4m3fn).view(np.uint8)
    words = codes.reshape(n // 512, 128, 4, m).transpose(0, 1, 3, 2)
    return np.ascontiguousarray(words), np.ascontiguousarray(byte.astype(np.uint8).reshape(n // 512, 16, m))


K, T, S, H, C = 512, 2048, 512, 512, 512


def setup_inputs():
    n = np.random.standard_normal
    s = mx_kscale(K)[:, None]
    packed_xT = pack_weight(n((K, T)) * s)
    packed_w1 = pack_weight(n((K, H)) / np.sqrt(K) / s)
    return {
        "x_words": packed_xT[0],
        "x_scales": packed_xT[1],
        "w1_words": packed_w1[0],
        "w1_scales": packed_w1[1],
        "sl": np.random.uniform(1.0, 2.0, (H, 1)).astype(np.float32),
        "th": (0.5 * n((H, 1))).astype(np.float32),
        "gs": (np.random.uniform(0.5, 1.5, (K, 1)) / s).astype(np.float32),
        "sl2": np.random.uniform(1.0, 2.0, (C, 1)).astype(np.float32),
        "th2": (0.5 * n((C, 1))).astype(np.float32),
        "offs": striped(np.random.permutation(T)[:S]),
        "n1": striped8(np.stack([np.random.permutation(S) for _ in range(8)])),
        "ca": striped(np.random.permutation(T)[:C]),
        "hc": striped8(np.random.randint(0, T, (8, C))),
        "n2": striped(np.random.permutation(S)),
        "n3": striped(np.random.permutation(S)),
    }


def reference(x_words, x_scales, w1_words, w1_scales, sl, th, gs, sl2, th2, offs, n1, ca, hc, n2, n3):
    x_ca = unpack_weight(x_words, x_scales)[:, unstriped(ca)]
    xq = unpack_weight(x_words, x_scales)[:, unstriped(offs)]
    y = unpack_weight(w1_words, w1_scales).T @ xq
    sg = sigmoid(f64(sl) * (y[np.arange(H)[:, None], runs(n1, H)] - f64(th)))
    z = f64(gs) * (y * sg)
    zq = mxq(z, 0, "e4m3")
    a = 0.0625 * (x_ca.T @ zq)
    x_hc = unpack_weight(x_words, x_scales)[np.arange(K)[:, None], runs(hc, K)]
    b = 0.0625 * (x_hc.T @ zq)
    sg2 = sigmoid(f64(sl2) * (b[:, unstriped(n2)] - f64(th2)))
    out_0 = a * sg2 - (0.5 * a[:, unstriped(n3)])
    return (out_0,) + planes(out_0)

@@ -1,0 +1,223 @@
+from contextlib import ExitStack
+
+import concourse.mybir as mybir
+
+K, T, S, H, C = 512, 2048, 512, 512, 512
+FLOPS = 3 * 2 * 512 * 512 * 512
+
+F32 = mybir.dt.float32
+BF16 = mybir.dt.bfloat16
+I32 = mybir.dt.int32
+U32 = mybir.dt.uint32
+U16 = mybir.dt.uint16
+U8 = mybir.dt.uint8
+FP8X4 = mybir.dt.float8_e4m3fn_x4
+MULT = mybir.AluOpType.mult
+ADD = mybir.AluOpType.add
+SIGMOID = mybir.ActivationFunctionType.Sigmoid
+COPY = mybir.ActivationFunctionType.Copy
+
+P = 128
+PACK = 4
+Z_WIDTHS = (256, 256,)
+OUT_WIDTHS = (256, 128, 128,)
+FETCH_ON_SCALAR = (False, True, True,)
+LIST_COLS = S // 16
+
+
+def tile_picked_cdhgxbesa_none_po_kernel(
+    tc, x_words, x_scales, w1_words, w1_scales, sl, th, gs, sl2, th2, offs, n1, ca, hc, n2, n3, out_0, out_1, out_2
+):
+    nc = tc.nc
+    with ExitStack() as ctx:
+        sb = ctx.enter_context(tc.tile_pool(name="sb", bufs=1))
+        ps = ctx.enter_context(tc.psum_pool(name="ps", bufs=1))
+
+        def tile(shape, dtype, name, tag=None):
+            return sb.tile(shape, dtype, name=name, tag=tag or name, align_bytes=64)
+
+        def load_list(src, name):
+            dst = tile([P, LIST_COLS], U16, name)
+            nc.sync.dma_start(dst[:], src)
+            return dst
+
+        def load_column(src, name):
+            dst = tile([P, PACK], F32, name)
+            nc.gpsimd.dma_start(dst[:], src.rearrange("(p t) o -> p (t o)", t=PACK))
+            return dst
+
+        def load_scale_rows(dst, src):
+            words = src.shape[2] // 4
+            for q in range(4):
+                rows = src[0, 4 * q : 4 * q + 4, :].bitcast(I32)
+                nc.sync.dma_start(dst[32 * q : 32 * q + 32, :].bitcast(I32), rows.unsqueeze(0).to_broadcast([8, 4, words]))
+
+        def dealt(ap):
+            return ap.rearrange("p (t m) -> p m t", t=PACK)
+
+        def in_order(ap):
+            return ap.rearrange("p (m t) -> p m t", t=PACK)
+
+        def chunks(widths):
+            return [slice(sum(widths[:c]), sum(widths[: c + 1])) for c in range(len(widths))]
+
+        def entries(lst, cols):
+            return lst[:, cols.start // 16 : cols.stop // 16]
+
+        def interleave(engine_copy, dst, src):
+            engine_copy(
+                dst.rearrange("p (c i) t -> p c t i", i=4),
+                src.rearrange("p t (c i) -> p c t i", i=4),
+            )
+
+        xs = tile([P, T], U8, "xs")
+        w1s = tile([P, H], U8, "w1s", tag="w1s_then_ca_w")
+        hc_s = tile([P, C], U8, "hc_s")
+        nc.vector.memset(hc_s[:].bitcast(I32), 0)
+
+        offs_t = load_list(offs, "offs_t")
+        load_scale_rows(xs, x_scales)
+        xw = tile([P, T], U32, "xw")
+        nc.sync.dma_start(xw[:].bitcast(I32), x_words[0].rearrange("p n t -> p (n t)").bitcast(I32))
+        ca_t = load_list(ca, "ca_t")
+        w1w = tile([P, H], U32, "w1w")
+        nc.sync.dma_start(w1w[:].bitcast(I32), w1_words[0].rearrange("p n t -> p (n t)").bitcast(I32))
+        load_scale_rows(w1s, w1_scales)
+        hc_t = load_list(hc, "hc_t")
+        n1_t = load_list(n1, "n1_t")
+        n2_t = load_list(n2, "n2_t")
+        n3_t = load_list(n3, "n3_t")
+        sl_t = load_column(sl, "sl_t")
+        th_t = load_column(th, "th_t")
+        gs_t = load_column(gs, "gs_t")
+        sl2_t = load_column(sl2, "sl2_t")
+        th2_t = load_column(th2, "th2_t")
+
+        xq_s = tile([P, S], U8, "xq_s")
+        nc.vector.tensor_copy(xq_s[:], xs[:].indirect(offs_t[:]))
+        w1w_d = tile([P, H], U32, "w1w_d")
+        nc.scalar.copy(dealt(w1w_d[:]), in_order(w1w[:]))
+        w1s_d = tile([P, H], U8, "w1s_d")
+        nc.vector.tensor_copy(dealt(w1s_d[:]), in_order(w1s[:]))
+        xq_w = tile([P, S], U32, "xq_w")
+        halves = chunks((S // 2, S // 2))
+        for cols in halves:
+            nc.vector.tensor_copy(xq_w[:, cols], xw[:].indirect(entries(offs_t, cols)))
+        ca_s = tile([P, C], U8, "ca_s")
+        nc.vector.tensor_copy(dealt(ca_s[:]), xs[:].indirect(ca_t[:]))
+
+        def product(bank, t, cols, lhs_w, lhs_s, rhs_w, rhs_s):
+            rows = slice(t * P, (t + 1) * P)
+            nc.tensor.matmul_mx(
+                bank[:, cols],
+                lhsT=lhs_w[:, rows].bitcast(FP8X4),
+                lhsT_scale=lhs_s[:, rows],
+                rhs=rhs_w[:, cols].bitcast(FP8X4),
+                rhs_scale=rhs_s[:, cols],
+                start=True,
+                stop=True,
+            )
+
+        y_ps = [ps.tile([P, S], F32, name=f"y_ps{t}", tag=f"bank{t}") for t in range(PACK)]
+        for t in range(PACK):
+            for cols in halves:
+                product(y_ps[t], t, cols, w1w_d, w1s_d, xq_w, xq_s)
+
+        def minus_product(u, v, name):
+            prod = tile([P, PACK], F32, name + "_p")
+            nc.gpsimd.tensor_tensor(prod[:], u[:], v[:], MULT)
+            neg = tile([P, PACK], F32, name)
+            nc.gpsimd.tensor_scalar(neg[:], prod[:], -1.0, 0.0, MULT, ADD)
+            return neg
+
+        bias1 = minus_product(sl_t, th_t, "bias1")
+        bias2 = minus_product(sl2_t, th2_t, "bias2")
+
+        def gate(dst, window, offsets, t, scale, bias):
+            nc.scalar.activation(
+                dst, window[:].indirect(offsets), SIGMOID, bias=bias[:, t : t + 1], scale=scale[:, t : t + 1]
+            )
+
+        def quantise(copy, src, width, words, scales, name):
+            woven = tile([P, width, PACK], BF16, name)
+            interleave(copy, woven[:], src[:])
+            nc.vector.quantize_mx(words.bitcast(FP8X4), scales, woven[:].rearrange("p c t -> p (c t)"))
+
+        y_sb = [tile([P, S], F32, f"y_sb{t}") for t in range(PACK)]
+        z_w = tile([P, S], U32, "z_w")
+        z_s = tile([P, S], U8, "z_s")
+        b_ps = [ps.tile([P, S], F32, name=f"b_ps{t}", tag=f"bank{PACK + t}") for t in range(PACK)]
+        b_sb = [tile([P, S], F32, f"b_sb{t}") for t in range(PACK)]
+        a_sb = [tile([P, S], F32, f"a_sb{t}") for t in range(PACK)]
+
+        def make_z(c, cols):
+            width = Z_WIDTHS[c]
+            sg = tile([P, PACK, width], F32, f"sg{c}")
+            z = tile([P, PACK, width], BF16, f"z{c}")
+            for t in range(PACK):
+                if c == 0:
+                    nc.scalar.copy(y_sb[t][:], y_ps[t][:])
+                gate(sg[:, t, :], y_sb[t], entries(n1_t, cols), t, sl_t, bias1)
+                nc.vector.scalar_tensor_tensor(z[:, t, :], y_ps[t][:, cols], gs_t[:, t : t + 1], sg[:, t, :], MULT, MULT)
+            quantise(nc.vector.tensor_copy, z, width, z_w[:, cols], z_s[:, cols], f"z_woven{c}")
+
+        z_chunks = chunks(Z_WIDTHS)
+        for c, cols in enumerate(z_chunks):
+            make_z(c, cols)
+
+        hc_s_g = tile([P, C], U8, "hc_s_g")
+        nc.vector.tensor_copy(hc_s_g[:], xs[:].indirect(hc_t[:]))
+        hc_s_d = tile([P, C], U8, "hc_s_d")
+        nc.vector.tensor_copy(dealt(hc_s_d[:]), in_order(hc_s_g[:]))
+        for r in range(4):
+            nc.sync.dma_start(hc_s[r:P:32, :].bitcast(I32), hc_s_d[16 * (r // 2) + r : P : 32, :].bitcast(I32))
+        hc_w_g = tile([P, C], U32, "hc_w_g")
+        nc.vector.tensor_copy(hc_w_g[:], xw[:].indirect(hc_t[:]))
+        hc_w = tile([P, C], U32, "hc_w")
+        nc.vector.tensor_copy(dealt(hc_w[:]), in_order(hc_w_g[:]))
+        ca_w = tile([P, C], U32, "ca_w", tag="w1s_then_ca_w")
+        nc.vector.tensor_copy(dealt(ca_w[:]), xw[:].indirect(ca_t[:]))
+
+        a_ps = [ps.tile([P, S], F32, name=f"a_ps{t}", tag=f"bank{t}") for t in range(PACK)]
+
+        def score_b(t, cols):
+            product(b_ps[t], t, cols, hc_w, hc_s, z_w, z_s)
+            nc.scalar.activation(b_sb[t][:, cols], b_ps[t][:, cols], COPY, scale=0.0625)
+
+        for cols in z_chunks[:-1]:
+            for t in range(PACK):
+                score_b(t, cols)
+            for t in range(PACK):
+                product(a_ps[t], t, cols, ca_w, ca_s, z_w, z_s)
+                nc.scalar.activation(a_sb[t][:, cols], a_ps[t][:, cols], COPY, scale=-0.03125)
+        cols = z_chunks[-1]
+        for t in range(PACK):
+            score_b(t, cols)
+            product(a_ps[t], t, cols, ca_w, ca_s, z_w, z_s)
+            nc.vector.tensor_scalar_mul(a_sb[t][:, cols], a_ps[t][:, cols], -0.03125)
+
+        res_w = tile([P, S], U32, "res_w")
+        res_s = tile([P, S], U8, "res_s")
+        out_rows = out_0.rearrange("(p t) c -> p t c", t=PACK)
+        out_words = out_1[0].rearrange("p n t -> p (n t)").bitcast(I32)
+        for c, cols in enumerate(chunks(OUT_WIDTHS)):
+            width = OUT_WIDTHS[c]
+            sg2 = tile([P, PACK, width], F32, f"sg2{c}")
+            gated = tile([P, PACK, width], F32, f"gated{c}")
+            fetched = tile([P, PACK, width], F32, f"fetched{c}")
+            res = tile([P, PACK, width], F32, f"res{c}")
+            for t in range(PACK):
+                looked_up = a_sb[t][:].indirect(entries(n3_t, cols))
+                if FETCH_ON_SCALAR[c]:
+                    nc.scalar.activation(fetched[:, t, :], looked_up, COPY)
+                else:
+                    nc.vector.tensor_copy(fetched[:, t, :], looked_up)
+                gate(sg2[:, t, :], b_sb[t], entries(n2_t, cols), t, sl2_t, bias2)
+                nc.vector.scalar_tensor_tensor(gated[:, t, :], a_ps[t][:, cols], 0.0625, sg2[:, t, :], MULT, MULT)
+                nc.gpsimd.tensor_tensor(res[:, t, :], fetched[:, t, :], gated[:, t, :], ADD)
+            nc.sync.dma_start(out_rows[:, :, cols], res[:])
+            quantise(nc.vector.tensor_copy, res, width, res_w[:, cols], res_s[:, cols], f"res_woven{c}")
+            nc.sync.dma_start(out_words[:, cols], res_w[:, cols].bitcast(I32))
+        for q in range(4):
+            queue = nc.scalar if q % 2 == 0 else nc.sync
+            queue.dma_start(out_2[0, 4 * q : 4 * q + 4, :].bitcast(I32), res_s[32 * q : 32 * q + 4, :].bitcast(I32))

@@ -19,7 +19,7 @@ COPY = mybir.ActivationFunctionType.Copy
 
 P = 128
 PACK = 4
-Z_WIDTHS = (256, 256,)
+Z_WIDTHS = (256, 128, 128,)
 OUT_WIDTHS = (256, 128, 128,)
 FETCH_ON_SCALAR = (False, True, True,)
 LIST_COLS = S // 16
@@ -41,9 +41,9 @@ def tile_picked_cdhgxbesa_none_po_kernel(
             nc.sync.dma_start(dst[:], src)
             return dst
 
-        def load_column(src, name):
+        def load_column(src, name, queue):
             dst = tile([P, PACK], F32, name)
-            nc.gpsimd.dma_start(dst[:], src.rearrange("(p t) o -> p (t o)", t=PACK))
+            queue.dma_start(dst[:], src.rearrange("(p t) o -> p (t o)", t=PACK))
             return dst
 
         def load_scale_rows(dst, src):
@@ -71,7 +71,7 @@ def tile_picked_cdhgxbesa_none_po_kernel(
             )
 
         xs = tile([P, T], U8, "xs")
-        w1s = tile([P, H], U8, "w1s", tag="w1s_then_ca_w")
+        w1s = tile([P, H], U8, "w1s", tag="staging")
         hc_s = tile([P, C], U8, "hc_s")
         nc.vector.memset(hc_s[:].bitcast(I32), 0)
 
@@ -87,12 +87,16 @@ def tile_picked_cdhgxbesa_none_po_kernel(
         n1_t = load_list(n1, "n1_t")
         n2_t = load_list(n2, "n2_t")
         n3_t = load_list(n3, "n3_t")
-        sl_t = load_column(sl, "sl_t")
-        th_t = load_column(th, "th_t")
-        gs_t = load_column(gs, "gs_t")
-        sl2_t = load_column(sl2, "sl2_t")
-        th2_t = load_column(th2, "th2_t")
+        sl_t = load_column(sl, "sl_t", nc.gpsimd)
+        th_t = load_column(th, "th_t", nc.gpsimd)
+        gs_t = load_column(gs, "gs_t", nc.gpsimd)
+        sl2_t = load_column(sl2, "sl2_t", nc.sync)
+        th2_t = load_column(th2, "th2_t", nc.sync)
 
+        warm_in = tile([P, 1], F32, "warm_in")
+        nc.vector.memset(warm_in[:], 0.0)
+        warm_out = tile([P, 1], F32, "warm_out")
+        nc.scalar.activation(warm_out[:], warm_in[:], SIGMOID)
         xq_s = tile([P, S], U8, "xq_s")
         nc.vector.tensor_copy(xq_s[:], xs[:].indirect(offs_t[:]))
         w1w_d = tile([P, H], U32, "w1w_d")
@@ -112,8 +116,8 @@ def tile_picked_cdhgxbesa_none_po_kernel(
                 bank[:, cols],
                 lhsT=lhs_w[:, rows].bitcast(FP8X4),
                 lhsT_scale=lhs_s[:, rows],
-                rhs=rhs_w[:, cols].bitcast(FP8X4),
-                rhs_scale=rhs_s[:, cols],
+                rhs=rhs_w.bitcast(FP8X4),
+                rhs_scale=rhs_s,
                 start=True,
                 stop=True,
             )
@@ -121,7 +125,7 @@ def tile_picked_cdhgxbesa_none_po_kernel(
         y_ps = [ps.tile([P, S], F32, name=f"y_ps{t}", tag=f"bank{t}") for t in range(PACK)]
         for t in range(PACK):
             for cols in halves:
-                product(y_ps[t], t, cols, w1w_d, w1s_d, xq_w, xq_s)
+                product(y_ps[t], t, cols, w1w_d, w1s_d, xq_w[:, cols], xq_s[:, cols])
 
         def minus_product(u, v, name):
             prod = tile([P, PACK], F32, name + "_p")
@@ -144,8 +148,8 @@ def tile_picked_cdhgxbesa_none_po_kernel(
             nc.vector.quantize_mx(words.bitcast(FP8X4), scales, woven[:].rearrange("p c t -> p (c t)"))
 
         y_sb = [tile([P, S], F32, f"y_sb{t}") for t in range(PACK)]
-        z_w = tile([P, S], U32, "z_w")
-        z_s = tile([P, S], U8, "z_s")
+        z_w = [tile([P, width], U32, f"z_w{c}") for c, width in enumerate(Z_WIDTHS)]
+        z_s = [tile([P, width], U8, f"z_s{c}") for c, width in enumerate(Z_WIDTHS)]
         b_ps = [ps.tile([P, S], F32, name=f"b_ps{t}", tag=f"bank{PACK + t}") for t in range(PACK)]
         b_sb = [tile([P, S], F32, f"b_sb{t}") for t in range(PACK)]
         a_sb = [tile([P, S], F32, f"a_sb{t}") for t in range(PACK)]
@@ -159,42 +163,47 @@ def tile_picked_cdhgxbesa_none_po_kernel(
                     nc.scalar.copy(y_sb[t][:], y_ps[t][:])
                 gate(sg[:, t, :], y_sb[t], entries(n1_t, cols), t, sl_t, bias1)
                 nc.vector.scalar_tensor_tensor(z[:, t, :], y_ps[t][:, cols], gs_t[:, t : t + 1], sg[:, t, :], MULT, MULT)
-            quantise(nc.vector.tensor_copy, z, width, z_w[:, cols], z_s[:, cols], f"z_woven{c}")
+            quantise(nc.vector.tensor_copy, z, width, z_w[c][:], z_s[c][:], f"z_woven{c}")
 
         z_chunks = chunks(Z_WIDTHS)
         for c, cols in enumerate(z_chunks):
             make_z(c, cols)
 
-        hc_s_g = tile([P, C], U8, "hc_s_g")
+        hc_s_g = tile([P, C], U8, "hc_s_g", tag="staging")
         nc.vector.tensor_copy(hc_s_g[:], xs[:].indirect(hc_t[:]))
         hc_s_d = tile([P, C], U8, "hc_s_d")
         nc.vector.tensor_copy(dealt(hc_s_d[:]), in_order(hc_s_g[:]))
         for r in range(4):
             nc.sync.dma_start(hc_s[r:P:32, :].bitcast(I32), hc_s_d[16 * (r // 2) + r : P : 32, :].bitcast(I32))
-        hc_w_g = tile([P, C], U32, "hc_w_g")
+        hc_w_g = tile([P, C], U32, "hc_w_g", tag="staging")
         nc.vector.tensor_copy(hc_w_g[:], xw[:].indirect(hc_t[:]))
         hc_w = tile([P, C], U32, "hc_w")
         nc.vector.tensor_copy(dealt(hc_w[:]), in_order(hc_w_g[:]))
-        ca_w = tile([P, C], U32, "ca_w", tag="w1s_then_ca_w")
+        ca_w = tile([P, C], U32, "ca_w", tag="staging")
         nc.vector.tensor_copy(dealt(ca_w[:]), xw[:].indirect(ca_t[:]))
 
         a_ps = [ps.tile([P, S], F32, name=f"a_ps{t}", tag=f"bank{t}") for t in range(PACK)]
 
-        def score_b(t, cols):
-            product(b_ps[t], t, cols, hc_w, hc_s, z_w, z_s)
-            nc.scalar.activation(b_sb[t][:, cols], b_ps[t][:, cols], COPY, scale=0.0625)
+        def score(banks, t, c, lhs_w, lhs_s):
+            product(banks[t], t, z_chunks[c], lhs_w, lhs_s, z_w[c][:], z_s[c][:])
 
-        for cols in z_chunks[:-1]:
-            for t in range(PACK):
-                score_b(t, cols)
-            for t in range(PACK):
-                product(a_ps[t], t, cols, ca_w, ca_s, z_w, z_s)
-                nc.scalar.activation(a_sb[t][:, cols], a_ps[t][:, cols], COPY, scale=-0.03125)
-        cols = z_chunks[-1]
+        first, rest = z_chunks[0], slice(Z_WIDTHS[0], S)
+        last = len(Z_WIDTHS) - 1
         for t in range(PACK):
-            score_b(t, cols)
-            product(a_ps[t], t, cols, ca_w, ca_s, z_w, z_s)
-            nc.vector.tensor_scalar_mul(a_sb[t][:, cols], a_ps[t][:, cols], -0.03125)
+            score(b_ps, t, 0, hc_w, hc_s)
+            nc.scalar.activation(b_sb[t][:, first], b_ps[t][:, first], COPY, scale=0.0625)
+        for t in range(PACK):
+            score(a_ps, t, 0, ca_w, ca_s)
+            nc.scalar.activation(a_sb[t][:, first], a_ps[t][:, first], COPY, scale=-0.03125)
+        for c in range(1, last):
+            for t in range(PACK):
+                score(b_ps, t, c, hc_w, hc_s)
+                score(a_ps, t, c, ca_w, ca_s)
+        for t in range(PACK):
+            score(b_ps, t, last, hc_w, hc_s)
+            nc.scalar.activation(b_sb[t][:, rest], b_ps[t][:, rest], COPY, scale=0.0625)
+            score(a_ps, t, last, ca_w, ca_s)
+            nc.vector.tensor_scalar_mul(a_sb[t][:, rest], a_ps[t][:, rest], -0.03125)
 
         res_w = tile([P, S], U32, "res_w")
         res_s = tile([P, S], U8, "res_s")
@@ -210,11 +219,12 @@ def tile_picked_cdhgxbesa_none_po_kernel(
                 looked_up = a_sb[t][:].indirect(entries(n3_t, cols))
                 if FETCH_ON_SCALAR[c]:
                     nc.scalar.activation(fetched[:, t, :], looked_up, COPY)
-                else:
-                    nc.vector.tensor_copy(fetched[:, t, :], looked_up)
                 gate(sg2[:, t, :], b_sb[t], entries(n2_t, cols), t, sl2_t, bias2)
                 nc.vector.scalar_tensor_tensor(gated[:, t, :], a_ps[t][:, cols], 0.0625, sg2[:, t, :], MULT, MULT)
-                nc.gpsimd.tensor_tensor(res[:, t, :], fetched[:, t, :], gated[:, t, :], ADD)
+                if FETCH_ON_SCALAR[c]:
+                    nc.vector.tensor_tensor(res[:, t, :], fetched[:, t, :], gated[:, t, :], ADD)
+                else:
+                    nc.vector.tensor_tensor(res[:, t, :], looked_up, gated[:, t, :], ADD)
             nc.sync.dma_start(out_rows[:, :, cols], res[:])
             quantise(nc.vector.tensor_copy, res, width, res_w[:, cols], res_s[:, cols], f"res_woven{c}")
             nc.sync.dma_start(out_words[:, cols], res_w[:, cols].bitcast(I32))

@@ -2,7 +2,7 @@ from contextlib import ExitStack
 
 import concourse.mybir as mybir
 
-K, T, S, H, C = 512, 2048, 512, 512, 512
+T, S, H, C = 2048, 512, 512, 512
 FLOPS = 3 * 2 * 512 * 512 * 512
 
 F32 = mybir.dt.float32
@@ -19,10 +19,12 @@ COPY = mybir.ActivationFunctionType.Copy
 
 P = 128
 PACK = 4
-Z_WIDTHS = (256, 128, 128,)
-OUT_WIDTHS = (256, 128, 128,)
-FETCH_ON_SCALAR = (False, True, True,)
-LIST_COLS = S // 16
+QUADRANT = 32
+GROUP = 16
+HALF = S // 2
+HALVES = (slice(0, HALF), slice(HALF, S))
+FETCHES_ON_VECTOR = 5
+WEAVE_RUN = 4
 
 
 def tile_picked_cdhgxbesa_none_po_kernel(
@@ -37,7 +39,7 @@ def tile_picked_cdhgxbesa_none_po_kernel(
             return sb.tile(shape, dtype, name=name, tag=tag or name, align_bytes=64)
 
         def load_list(src, name):
-            dst = tile([P, LIST_COLS], U16, name)
+            dst = tile([P, S // GROUP], U16, name)
             nc.sync.dma_start(dst[:], src)
             return dst
 
@@ -46,11 +48,14 @@ def tile_picked_cdhgxbesa_none_po_kernel(
             queue.dma_start(dst[:], src.rearrange("(p t) o -> p (t o)", t=PACK))
             return dst
 
-        def load_scale_rows(dst, src):
-            words = src.shape[2] // 4
-            for q in range(4):
+        def load_words(src, dst):
+            nc.sync.dma_start(dst[:].bitcast(I32), src[0].rearrange("p n t -> p (n t)").bitcast(I32))
+
+        def load_scale_rows(src, dst):
+            for q in range(P // QUADRANT):
                 rows = src[0, 4 * q : 4 * q + 4, :].bitcast(I32)
-                nc.sync.dma_start(dst[32 * q : 32 * q + 32, :].bitcast(I32), rows.unsqueeze(0).to_broadcast([8, 4, words]))
+                repeated = rows.unsqueeze(0).to_broadcast([QUADRANT // 4, 4, src.shape[2] // 4])
+                nc.sync.dma_start(dst[QUADRANT * q : QUADRANT * (q + 1), :].bitcast(I32), repeated)
 
         def dealt(ap):
             return ap.rearrange("p (t m) -> p m t", t=PACK)
@@ -58,33 +63,58 @@ def tile_picked_cdhgxbesa_none_po_kernel(
         def in_order(ap):
             return ap.rearrange("p (m t) -> p m t", t=PACK)
 
-        def chunks(widths):
-            return [slice(sum(widths[:c]), sum(widths[: c + 1])) for c in range(len(widths))]
-
         def entries(lst, cols):
-            return lst[:, cols.start // 16 : cols.stop // 16]
+            return lst[:, cols.start // GROUP : cols.stop // GROUP]
 
-        def interleave(engine_copy, dst, src):
-            engine_copy(
-                dst.rearrange("p (c i) t -> p c t i", i=4),
-                src.rearrange("p t (c i) -> p c t i", i=4),
+        def product(out, t, lhs_w, lhs_s, rhs_w, rhs_s):
+            rows = slice(t * P, (t + 1) * P)
+            nc.tensor.matmul_mx(
+                out,
+                lhsT=lhs_w[:, rows].bitcast(FP8X4),
+                lhsT_scale=lhs_s[:, rows],
+                rhs=rhs_w.bitcast(FP8X4),
+                rhs_scale=rhs_s,
+                start=True,
+                stop=True,
             )
 
+        def minus_product(u, v, name):
+            prod = tile([P, PACK], F32, name + "_negated")
+            nc.gpsimd.tensor_tensor(prod[:], u[:], v[:], MULT)
+            neg = tile([P, PACK], F32, name)
+            nc.gpsimd.tensor_scalar(neg[:], prod[:], -1.0, 0.0, MULT, ADD)
+            return neg
+
+        def gate(dst, window, offsets, t, scale, bias):
+            nc.scalar.activation(
+                dst, window[:].indirect(offsets), SIGMOID, bias=bias[:, t : t + 1], scale=scale[:, t : t + 1]
+            )
+
+        def quantise(src, words, scales, name):
+            woven = tile([P, HALF, PACK], BF16, name)
+            nc.vector.tensor_copy(
+                woven[:].rearrange("p (c i) t -> p c t i", i=WEAVE_RUN),
+                src[:].rearrange("p t (c i) -> p c t i", i=WEAVE_RUN),
+            )
+            nc.vector.quantize_mx(words.bitcast(FP8X4), scales, woven[:].rearrange("p c t -> p (c t)"))
+
+        first_w1s, first_w1w, first_hc_s = "w1s_hc_w_ca_w", "w1w_hc_s", "hc_s_ca_s"
+
         xs = tile([P, T], U8, "xs")
-        w1s = tile([P, H], U8, "w1s", tag="staging")
+        w1s = tile([P, H], U8, "w1s", tag=first_w1s)
         hc_s = tile([P, C], U8, "hc_s")
         nc.vector.memset(hc_s[:].bitcast(I32), 0)
 
+        load_scale_rows(x_scales, xs)
         offs_t = load_list(offs, "offs_t")
-        load_scale_rows(xs, x_scales)
-        xw = tile([P, T], U32, "xw")
-        nc.sync.dma_start(xw[:].bitcast(I32), x_words[0].rearrange("p n t -> p (n t)").bitcast(I32))
-        ca_t = load_list(ca, "ca_t")
-        w1w = tile([P, H], U32, "w1w")
-        nc.sync.dma_start(w1w[:].bitcast(I32), w1_words[0].rearrange("p n t -> p (n t)").bitcast(I32))
-        load_scale_rows(w1s, w1_scales)
         hc_t = load_list(hc, "hc_t")
+        xw = tile([P, T], U32, "xw")
+        load_words(x_words, xw)
+        w1w = tile([P, H], U32, "w1w", tag=first_w1w)
+        load_words(w1_words, w1w)
+        load_scale_rows(w1_scales, w1s)
         n1_t = load_list(n1, "n1_t")
+        ca_t = load_list(ca, "ca_t")
         n2_t = load_list(n2, "n2_t")
         n3_t = load_list(n3, "n3_t")
         sl_t = load_column(sl, "sl_t", nc.gpsimd)
@@ -97,6 +127,7 @@ def tile_picked_cdhgxbesa_none_po_kernel(
         nc.vector.memset(warm_in[:], 0.0)
         warm_out = tile([P, 1], F32, "warm_out")
         nc.scalar.activation(warm_out[:], warm_in[:], SIGMOID)
+
         xq_s = tile([P, S], U8, "xq_s")
         nc.vector.tensor_copy(xq_s[:], xs[:].indirect(offs_t[:]))
         w1w_d = tile([P, H], U32, "w1w_d")
@@ -104,130 +135,90 @@ def tile_picked_cdhgxbesa_none_po_kernel(
         w1s_d = tile([P, H], U8, "w1s_d")
         nc.vector.tensor_copy(dealt(w1s_d[:]), in_order(w1s[:]))
         xq_w = tile([P, S], U32, "xq_w")
-        halves = chunks((S // 2, S // 2))
-        for cols in halves:
-            nc.vector.tensor_copy(xq_w[:, cols], xw[:].indirect(entries(offs_t, cols)))
-        ca_s = tile([P, C], U8, "ca_s")
-        nc.vector.tensor_copy(dealt(ca_s[:]), xs[:].indirect(ca_t[:]))
-
-        def product(bank, t, cols, lhs_w, lhs_s, rhs_w, rhs_s):
-            rows = slice(t * P, (t + 1) * P)
-            nc.tensor.matmul_mx(
-                bank[:, cols],
-                lhsT=lhs_w[:, rows].bitcast(FP8X4),
-                lhsT_scale=lhs_s[:, rows],
-                rhs=rhs_w.bitcast(FP8X4),
-                rhs_scale=rhs_s,
-                start=True,
-                stop=True,
-            )
-
+        nc.vector.tensor_copy(xq_w[:], xw[:].indirect(offs_t[:]))
         y_ps = [ps.tile([P, S], F32, name=f"y_ps{t}", tag=f"bank{t}") for t in range(PACK)]
         for t in range(PACK):
-            for cols in halves:
-                product(y_ps[t], t, cols, w1w_d, w1s_d, xq_w[:, cols], xq_s[:, cols])
-
-        def minus_product(u, v, name):
-            prod = tile([P, PACK], F32, name + "_p")
-            nc.gpsimd.tensor_tensor(prod[:], u[:], v[:], MULT)
-            neg = tile([P, PACK], F32, name)
-            nc.gpsimd.tensor_scalar(neg[:], prod[:], -1.0, 0.0, MULT, ADD)
-            return neg
+            product(y_ps[t][:], t, w1w_d, w1s_d, xq_w[:], xq_s[:])
 
         bias1 = minus_product(sl_t, th_t, "bias1")
         bias2 = minus_product(sl2_t, th2_t, "bias2")
 
-        def gate(dst, window, offsets, t, scale, bias):
-            nc.scalar.activation(
-                dst, window[:].indirect(offsets), SIGMOID, bias=bias[:, t : t + 1], scale=scale[:, t : t + 1]
-            )
-
-        def quantise(copy, src, width, words, scales, name):
-            woven = tile([P, width, PACK], BF16, name)
-            interleave(copy, woven[:], src[:])
-            nc.vector.quantize_mx(words.bitcast(FP8X4), scales, woven[:].rearrange("p c t -> p (c t)"))
-
         y_sb = [tile([P, S], F32, f"y_sb{t}") for t in range(PACK)]
-        z_w = [tile([P, width], U32, f"z_w{c}") for c, width in enumerate(Z_WIDTHS)]
-        z_s = [tile([P, width], U8, f"z_s{c}") for c, width in enumerate(Z_WIDTHS)]
+        z_w = [tile([P, HALF], U32, f"z_w{h}") for h in range(len(HALVES))]
+        z_s = [tile([P, HALF], U8, f"z_s{h}") for h in range(len(HALVES))]
         b_ps = [ps.tile([P, S], F32, name=f"b_ps{t}", tag=f"bank{PACK + t}") for t in range(PACK)]
         b_sb = [tile([P, S], F32, f"b_sb{t}") for t in range(PACK)]
         a_sb = [tile([P, S], F32, f"a_sb{t}") for t in range(PACK)]
-
-        def make_z(c, cols):
-            width = Z_WIDTHS[c]
-            sg = tile([P, PACK, width], F32, f"sg{c}")
-            z = tile([P, PACK, width], BF16, f"z{c}")
+        for h, cols in enumerate(HALVES):
+            sg = tile([P, PACK, HALF], F32, f"sg{h}")
+            z = tile([P, PACK, HALF], BF16, f"z{h}")
             for t in range(PACK):
-                if c == 0:
+                if h == 0:
                     nc.scalar.copy(y_sb[t][:], y_ps[t][:])
                 gate(sg[:, t, :], y_sb[t], entries(n1_t, cols), t, sl_t, bias1)
                 nc.vector.scalar_tensor_tensor(z[:, t, :], y_ps[t][:, cols], gs_t[:, t : t + 1], sg[:, t, :], MULT, MULT)
-            quantise(nc.vector.tensor_copy, z, width, z_w[c][:], z_s[c][:], f"z_woven{c}")
+            quantise(z, z_w[h][:], z_s[h][:], f"z_woven{h}")
 
-        z_chunks = chunks(Z_WIDTHS)
-        for c, cols in enumerate(z_chunks):
-            make_z(c, cols)
-
-        hc_s_g = tile([P, C], U8, "hc_s_g", tag="staging")
+        hc_s_g = tile([P, C], U8, "hc_s_g", tag=first_hc_s)
         nc.vector.tensor_copy(hc_s_g[:], xs[:].indirect(hc_t[:]))
-        hc_s_d = tile([P, C], U8, "hc_s_d")
+        hc_s_d = tile([P, C], U8, "hc_s_d", tag=first_w1w)
         nc.vector.tensor_copy(dealt(hc_s_d[:]), in_order(hc_s_g[:]))
         for r in range(4):
-            nc.sync.dma_start(hc_s[r:P:32, :].bitcast(I32), hc_s_d[16 * (r // 2) + r : P : 32, :].bitcast(I32))
-        hc_w_g = tile([P, C], U32, "hc_w_g", tag="staging")
+            source = GROUP * (r // 2) + r
+            nc.sync.dma_start(hc_s[r:P:QUADRANT, :].bitcast(I32), hc_s_d[source:P:QUADRANT, :].bitcast(I32))
+        hc_w_g = tile([P, C], U32, "hc_w_g", tag=first_w1s)
         nc.vector.tensor_copy(hc_w_g[:], xw[:].indirect(hc_t[:]))
         hc_w = tile([P, C], U32, "hc_w")
         nc.vector.tensor_copy(dealt(hc_w[:]), in_order(hc_w_g[:]))
-        ca_w = tile([P, C], U32, "ca_w", tag="staging")
+        ca_w = tile([P, C], U32, "ca_w", tag=first_w1s)
         nc.vector.tensor_copy(dealt(ca_w[:]), xw[:].indirect(ca_t[:]))
+        ca_s = tile([P, C], U8, "ca_s", tag=first_hc_s)
+        nc.vector.tensor_copy(dealt(ca_s[:]), xs[:].indirect(ca_t[:]))
 
         a_ps = [ps.tile([P, S], F32, name=f"a_ps{t}", tag=f"bank{t}") for t in range(PACK)]
 
-        def score(banks, t, c, lhs_w, lhs_s):
-            product(banks[t], t, z_chunks[c], lhs_w, lhs_s, z_w[c][:], z_s[c][:])
+        def score_b(t, h):
+            product(b_ps[t][:, HALVES[h]], t, hc_w, hc_s, z_w[h][:], z_s[h][:])
+            nc.scalar.activation(b_sb[t][:, HALVES[h]], b_ps[t][:, HALVES[h]], COPY, scale=0.0625)
 
-        first, rest = z_chunks[0], slice(Z_WIDTHS[0], S)
-        last = len(Z_WIDTHS) - 1
+        def score_a(t, h):
+            product(a_ps[t][:, HALVES[h]], t, ca_w, ca_s, z_w[h][:], z_s[h][:])
+
+        minus_half_a = -0.5 * 0.0625
         for t in range(PACK):
-            score(b_ps, t, 0, hc_w, hc_s)
-            nc.scalar.activation(b_sb[t][:, first], b_ps[t][:, first], COPY, scale=0.0625)
+            score_b(t, 0)
         for t in range(PACK):
-            score(a_ps, t, 0, ca_w, ca_s)
-            nc.scalar.activation(a_sb[t][:, first], a_ps[t][:, first], COPY, scale=-0.03125)
-        for c in range(1, last):
-            for t in range(PACK):
-                score(b_ps, t, c, hc_w, hc_s)
-                score(a_ps, t, c, ca_w, ca_s)
+            score_a(t, 0)
+            nc.scalar.activation(a_sb[t][:, HALVES[0]], a_ps[t][:, HALVES[0]], COPY, scale=minus_half_a)
         for t in range(PACK):
-            score(b_ps, t, last, hc_w, hc_s)
-            nc.scalar.activation(b_sb[t][:, rest], b_ps[t][:, rest], COPY, scale=0.0625)
-            score(a_ps, t, last, ca_w, ca_s)
-            nc.vector.tensor_scalar_mul(a_sb[t][:, rest], a_ps[t][:, rest], -0.03125)
+            score_b(t, 1)
+            score_a(t, 1)
+            nc.vector.tensor_scalar_mul(a_sb[t][:, HALVES[1]], a_ps[t][:, HALVES[1]], minus_half_a)
 
         res_w = tile([P, S], U32, "res_w")
         res_s = tile([P, S], U8, "res_s")
         out_rows = out_0.rearrange("(p t) c -> p t c", t=PACK)
         out_words = out_1[0].rearrange("p n t -> p (n t)").bitcast(I32)
-        for c, cols in enumerate(chunks(OUT_WIDTHS)):
-            width = OUT_WIDTHS[c]
-            sg2 = tile([P, PACK, width], F32, f"sg2{c}")
-            gated = tile([P, PACK, width], F32, f"gated{c}")
-            fetched = tile([P, PACK, width], F32, f"fetched{c}")
-            res = tile([P, PACK, width], F32, f"res{c}")
+        for h, cols in enumerate(HALVES):
+            sg2 = tile([P, PACK, HALF], F32, f"sg2_{h}")
+            gated = tile([P, PACK, HALF], F32, f"gated{h}")
+            fetched = tile([P, PACK, HALF], F32, f"fetched{h}")
+            res = tile([P, PACK, HALF], F32, f"res{h}")
             for t in range(PACK):
                 looked_up = a_sb[t][:].indirect(entries(n3_t, cols))
-                if FETCH_ON_SCALAR[c]:
+                if PACK * h + t < FETCHES_ON_VECTOR:
+                    nc.vector.tensor_copy(fetched[:, t, :], looked_up)
+                else:
                     nc.scalar.activation(fetched[:, t, :], looked_up, COPY)
                 gate(sg2[:, t, :], b_sb[t], entries(n2_t, cols), t, sl2_t, bias2)
                 nc.vector.scalar_tensor_tensor(gated[:, t, :], a_ps[t][:, cols], 0.0625, sg2[:, t, :], MULT, MULT)
-                if FETCH_ON_SCALAR[c]:
-                    nc.vector.tensor_tensor(res[:, t, :], fetched[:, t, :], gated[:, t, :], ADD)
-                else:
-                    nc.vector.tensor_tensor(res[:, t, :], looked_up, gated[:, t, :], ADD)
+            sums = [slice(0, PACK)] if h == 0 else [slice(0, PACK - 1), slice(PACK - 1, PACK)]
+            for ts in sums:
+                nc.vector.tensor_tensor(res[:, ts, :], fetched[:, ts, :], gated[:, ts, :], ADD)
             nc.sync.dma_start(out_rows[:, :, cols], res[:])
-            quantise(nc.vector.tensor_copy, res, width, res_w[:, cols], res_s[:, cols], f"res_woven{c}")
+            quantise(res, res_w[:, cols], res_s[:, cols], f"res_woven{h}")
             nc.sync.dma_start(out_words[:, cols], res_w[:, cols].bitcast(I32))
-        for q in range(4):
+        for q in range(P // QUADRANT):
             queue = nc.scalar if q % 2 == 0 else nc.sync
-            queue.dma_start(out_2[0, 4 * q : 4 * q + 4, :].bitcast(I32), res_s[32 * q : 32 * q + 4, :].bitcast(I32))
+            live = res_s[QUADRANT * q : QUADRANT * q + 4, :]
+            queue.dma_start(out_2[0, 4 * q : 4 * q + 4, :].bitcast(I32), live.bitcast(I32))

@@ -63,6 +63,11 @@ def tile_picked_cdhgxbesa_none_po_kernel(
         def in_order(ap):
             return ap.rearrange("p (m t) -> p m t", t=PACK)
 
+        def deal_bytes(dst, src):
+            nc.vector.tensor_copy(
+                dst[:].rearrange("p (t m) -> p t m", t=PACK), src[:].rearrange("p (m t) -> p t m", t=PACK)
+            )
+
         def entries(lst, cols):
             return lst[:, cols.start // GROUP : cols.stop // GROUP]
 
@@ -133,7 +138,7 @@ def tile_picked_cdhgxbesa_none_po_kernel(
         w1w_d = tile([P, H], U32, "w1w_d")
         nc.scalar.copy(dealt(w1w_d[:]), in_order(w1w[:]))
         w1s_d = tile([P, H], U8, "w1s_d")
-        nc.vector.tensor_copy(dealt(w1s_d[:]), in_order(w1s[:]))
+        deal_bytes(w1s_d, w1s)
         xq_w = tile([P, S], U32, "xq_w")
         nc.vector.tensor_copy(xq_w[:], xw[:].indirect(offs_t[:]))
         y_ps = [ps.tile([P, S], F32, name=f"y_ps{t}", tag=f"bank{t}") for t in range(PACK)]
@@ -151,7 +156,7 @@ def tile_picked_cdhgxbesa_none_po_kernel(
         a_sb = [tile([P, S], F32, f"a_sb{t}") for t in range(PACK)]
         for h, cols in enumerate(HALVES):
             sg = tile([P, PACK, HALF], F32, f"sg{h}")
-            z = tile([P, PACK, HALF], BF16, f"z{h}")
+            z = tile([P, PACK, HALF], BF16, f"z{h}", tag="z")
             for t in range(PACK):
                 if h == 0:
                     nc.scalar.copy(y_sb[t][:], y_ps[t][:])
@@ -162,7 +167,7 @@ def tile_picked_cdhgxbesa_none_po_kernel(
         hc_s_g = tile([P, C], U8, "hc_s_g", tag=first_hc_s)
         nc.vector.tensor_copy(hc_s_g[:], xs[:].indirect(hc_t[:]))
         hc_s_d = tile([P, C], U8, "hc_s_d", tag=first_w1w)
-        nc.vector.tensor_copy(dealt(hc_s_d[:]), in_order(hc_s_g[:]))
+        deal_bytes(hc_s_d, hc_s_g)
         for r in range(4):
             source = GROUP * (r // 2) + r
             nc.sync.dma_start(hc_s[r:P:QUADRANT, :].bitcast(I32), hc_s_d[source:P:QUADRANT, :].bitcast(I32))
@@ -170,10 +175,14 @@ def tile_picked_cdhgxbesa_none_po_kernel(
         nc.vector.tensor_copy(hc_w_g[:], xw[:].indirect(hc_t[:]))
         hc_w = tile([P, C], U32, "hc_w")
         nc.vector.tensor_copy(dealt(hc_w[:]), in_order(hc_w_g[:]))
-        ca_w = tile([P, C], U32, "ca_w", tag=first_w1s)
-        nc.vector.tensor_copy(dealt(ca_w[:]), xw[:].indirect(ca_t[:]))
-        ca_s = tile([P, C], U8, "ca_s", tag=first_hc_s)
-        nc.vector.tensor_copy(dealt(ca_s[:]), xs[:].indirect(ca_t[:]))
+        ca_w_g = tile([P, C], U32, "ca_w_g", tag=first_w1s)
+        nc.vector.tensor_copy(ca_w_g[:], xw[:].indirect(ca_t[:]))
+        ca_w = tile([P, C], U32, "ca_w")
+        nc.vector.tensor_copy(dealt(ca_w[:]), in_order(ca_w_g[:]))
+        ca_s_g = tile([P, C], U8, "ca_s_g", tag=first_hc_s)
+        nc.vector.tensor_copy(ca_s_g[:], xs[:].indirect(ca_t[:]))
+        ca_s = tile([P, C], U8, "ca_s")
+        deal_bytes(ca_s, ca_s_g)
 
         a_ps = [ps.tile([P, S], F32, name=f"a_ps{t}", tag=f"bank{t}") for t in range(PACK)]
 
@@ -199,22 +208,23 @@ def tile_picked_cdhgxbesa_none_po_kernel(
         res_s = tile([P, S], U8, "res_s")
         out_rows = out_0.rearrange("(p t) c -> p t c", t=PACK)
         out_words = out_1[0].rearrange("p n t -> p (n t)").bitcast(I32)
+        fetched = tile([P, PACK, HALF], F32, "fetched")
         for h, cols in enumerate(HALVES):
             sg2 = tile([P, PACK, HALF], F32, f"sg2_{h}")
             gated = tile([P, PACK, HALF], F32, f"gated{h}")
-            fetched = tile([P, PACK, HALF], F32, f"fetched{h}")
             res = tile([P, PACK, HALF], F32, f"res{h}")
+            fused = min(PACK, FETCHES_ON_VECTOR - PACK * h)
             for t in range(PACK):
                 looked_up = a_sb[t][:].indirect(entries(n3_t, cols))
-                if PACK * h + t < FETCHES_ON_VECTOR:
-                    nc.vector.tensor_copy(fetched[:, t, :], looked_up)
-                else:
+                if t >= fused:
                     nc.scalar.activation(fetched[:, t, :], looked_up, COPY)
                 gate(sg2[:, t, :], b_sb[t], entries(n2_t, cols), t, sl2_t, bias2)
                 nc.vector.scalar_tensor_tensor(gated[:, t, :], a_ps[t][:, cols], 0.0625, sg2[:, t, :], MULT, MULT)
-            sums = [slice(0, PACK)] if h == 0 else [slice(0, PACK - 1), slice(PACK - 1, PACK)]
-            for ts in sums:
-                nc.vector.tensor_tensor(res[:, ts, :], fetched[:, ts, :], gated[:, ts, :], ADD)
+                if t < fused:
+                    nc.vector.tensor_tensor(res[:, t, :], looked_up, gated[:, t, :], ADD)
+            if fused < PACK:
+                for ts in (slice(fused, PACK - 1), slice(PACK - 1, PACK)):
+                    nc.vector.tensor_tensor(res[:, ts, :], fetched[:, ts, :], gated[:, ts, :], ADD)
             nc.sync.dma_start(out_rows[:, :, cols], res[:])
             quantise(res, res_w[:, cols], res_s[:, cols], f"res_woven{h}")
             nc.sync.dma_start(out_words[:, cols], res_w[:, cols].bitcast(I32))

from contextlib import ExitStack

import concourse.mybir as mybir

T, S, H, C = 2048, 512, 512, 512
FLOPS = 3 * 2 * 512 * 512 * 512

F32 = mybir.dt.float32
BF16 = mybir.dt.bfloat16
I32 = mybir.dt.int32
U32 = mybir.dt.uint32
U16 = mybir.dt.uint16
U8 = mybir.dt.uint8
FP8X4 = mybir.dt.float8_e4m3fn_x4
MULT = mybir.AluOpType.mult
ADD = mybir.AluOpType.add
SIGMOID = mybir.ActivationFunctionType.Sigmoid
COPY = mybir.ActivationFunctionType.Copy

P = 128
PACK = 4
QUADRANT = 32
GROUP = 16
HALF = S // 2
HALVES = (slice(0, HALF), slice(HALF, S))
FETCHES_ON_VECTOR = 5
WEAVE_RUN = 4


def tile_picked_cdhgxbesa_none_po_kernel(
    tc, x_words, x_scales, w1_words, w1_scales, sl, th, gs, sl2, th2, offs, n1, ca, hc, n2, n3, out_0, out_1, out_2
):
    nc = tc.nc
    with ExitStack() as ctx:
        sb = ctx.enter_context(tc.tile_pool(name="sb", bufs=1))
        ps = ctx.enter_context(tc.psum_pool(name="ps", bufs=1))

        def tile(shape, dtype, name, tag=None):
            return sb.tile(shape, dtype, name=name, tag=tag or name, align_bytes=64)

        def load_list(src, name):
            dst = tile([P, S // GROUP], U16, name)
            nc.sync.dma_start(dst[:], src)
            return dst

        def load_column(src, name, queue):
            dst = tile([P, PACK], F32, name)
            queue.dma_start(dst[:], src.rearrange("(p t) o -> p (t o)", t=PACK))
            return dst

        def load_words(src, dst):
            nc.sync.dma_start(dst[:].bitcast(I32), src[0].rearrange("p n t -> p (n t)").bitcast(I32))

        def load_scale_rows(src, dst):
            for q in range(P // QUADRANT):
                rows = src[0, 4 * q : 4 * q + 4, :].bitcast(I32)
                repeated = rows.unsqueeze(0).to_broadcast([QUADRANT // 4, 4, src.shape[2] // 4])
                nc.sync.dma_start(dst[QUADRANT * q : QUADRANT * (q + 1), :].bitcast(I32), repeated)

        def dealt(ap):
            return ap.rearrange("p (t m) -> p m t", t=PACK)

        def in_order(ap):
            return ap.rearrange("p (m t) -> p m t", t=PACK)

        def deal_bytes(dst, src):
            nc.vector.tensor_copy(
                dst[:].rearrange("p (t m) -> p t m", t=PACK), src[:].rearrange("p (m t) -> p t m", t=PACK)
            )

        def entries(lst, cols):
            return lst[:, cols.start // GROUP : cols.stop // GROUP]

        def product(out, t, lhs_w, lhs_s, rhs_w, rhs_s):
            rows = slice(t * P, (t + 1) * P)
            nc.tensor.matmul_mx(
                out,
                lhsT=lhs_w[:, rows].bitcast(FP8X4),
                lhsT_scale=lhs_s[:, rows],
                rhs=rhs_w.bitcast(FP8X4),
                rhs_scale=rhs_s,
                start=True,
                stop=True,
            )

        def minus_product(u, v, name):
            prod = tile([P, PACK], F32, name + "_negated")
            nc.gpsimd.tensor_tensor(prod[:], u[:], v[:], MULT)
            neg = tile([P, PACK], F32, name)
            nc.gpsimd.tensor_scalar(neg[:], prod[:], -1.0, 0.0, MULT, ADD)
            return neg

        def gate(dst, window, offsets, t, scale, bias):
            nc.scalar.activation(
                dst, window[:].indirect(offsets), SIGMOID, bias=bias[:, t : t + 1], scale=scale[:, t : t + 1]
            )

        def quantise(src, words, scales, name):
            woven = tile([P, HALF, PACK], BF16, name)
            nc.vector.tensor_copy(
                woven[:].rearrange("p (c i) t -> p c t i", i=WEAVE_RUN),
                src[:].rearrange("p t (c i) -> p c t i", i=WEAVE_RUN),
            )
            nc.vector.quantize_mx(words.bitcast(FP8X4), scales, woven[:].rearrange("p c t -> p (c t)"))

        first_w1s, first_w1w, first_hc_s = "w1s_hc_w_ca_w", "w1w_hc_s", "hc_s_ca_s"

        xs = tile([P, T], U8, "xs")
        w1s = tile([P, H], U8, "w1s", tag=first_w1s)
        hc_s = tile([P, C], U8, "hc_s")
        nc.vector.memset(hc_s[:].bitcast(I32), 0)

        load_scale_rows(x_scales, xs)
        offs_t = load_list(offs, "offs_t")
        hc_t = load_list(hc, "hc_t")
        xw = tile([P, T], U32, "xw")
        load_words(x_words, xw)
        w1w = tile([P, H], U32, "w1w", tag=first_w1w)
        load_words(w1_words, w1w)
        load_scale_rows(w1_scales, w1s)
        n1_t = load_list(n1, "n1_t")
        ca_t = load_list(ca, "ca_t")
        n2_t = load_list(n2, "n2_t")
        n3_t = load_list(n3, "n3_t")
        sl_t = load_column(sl, "sl_t", nc.gpsimd)
        th_t = load_column(th, "th_t", nc.gpsimd)
        gs_t = load_column(gs, "gs_t", nc.gpsimd)
        sl2_t = load_column(sl2, "sl2_t", nc.sync)
        th2_t = load_column(th2, "th2_t", nc.sync)

        warm_in = tile([P, 1], F32, "warm_in")
        nc.vector.memset(warm_in[:], 0.0)
        warm_out = tile([P, 1], F32, "warm_out")
        nc.scalar.activation(warm_out[:], warm_in[:], SIGMOID)

        xq_s = tile([P, S], U8, "xq_s")
        nc.vector.tensor_copy(xq_s[:], xs[:].indirect(offs_t[:]))
        w1w_d = tile([P, H], U32, "w1w_d")
        nc.scalar.copy(dealt(w1w_d[:]), in_order(w1w[:]))
        w1s_d = tile([P, H], U8, "w1s_d")
        deal_bytes(w1s_d, w1s)
        xq_w = tile([P, S], U32, "xq_w")
        nc.vector.tensor_copy(xq_w[:], xw[:].indirect(offs_t[:]))
        y_ps = [ps.tile([P, S], F32, name=f"y_ps{t}", tag=f"bank{t}") for t in range(PACK)]
        for t in range(PACK):
            product(y_ps[t][:], t, w1w_d, w1s_d, xq_w[:], xq_s[:])

        bias1 = minus_product(sl_t, th_t, "bias1")
        bias2 = minus_product(sl2_t, th2_t, "bias2")

        y_sb = [tile([P, S], F32, f"y_sb{t}") for t in range(PACK)]
        z_w = [tile([P, HALF], U32, f"z_w{h}") for h in range(len(HALVES))]
        z_s = [tile([P, HALF], U8, f"z_s{h}") for h in range(len(HALVES))]
        b_ps = [ps.tile([P, S], F32, name=f"b_ps{t}", tag=f"bank{PACK + t}") for t in range(PACK)]
        b_sb = [tile([P, S], F32, f"b_sb{t}") for t in range(PACK)]
        a_sb = [tile([P, S], F32, f"a_sb{t}") for t in range(PACK)]
        for h, cols in enumerate(HALVES):
            sg = tile([P, PACK, HALF], F32, f"sg{h}")
            z = tile([P, PACK, HALF], BF16, f"z{h}", tag="z")
            for t in range(PACK):
                if h == 0:
                    nc.scalar.copy(y_sb[t][:], y_ps[t][:])
                gate(sg[:, t, :], y_sb[t], entries(n1_t, cols), t, sl_t, bias1)
                nc.vector.scalar_tensor_tensor(z[:, t, :], y_ps[t][:, cols], gs_t[:, t : t + 1], sg[:, t, :], MULT, MULT)
            quantise(z, z_w[h][:], z_s[h][:], f"z_woven{h}")

        hc_s_g = tile([P, C], U8, "hc_s_g", tag=first_hc_s)
        nc.vector.tensor_copy(hc_s_g[:], xs[:].indirect(hc_t[:]))
        hc_s_d = tile([P, C], U8, "hc_s_d", tag=first_w1w)
        deal_bytes(hc_s_d, hc_s_g)
        for r in range(4):
            source = GROUP * (r // 2) + r
            nc.sync.dma_start(hc_s[r:P:QUADRANT, :].bitcast(I32), hc_s_d[source:P:QUADRANT, :].bitcast(I32))
        hc_w_g = tile([P, C], U32, "hc_w_g", tag=first_w1s)
        nc.vector.tensor_copy(hc_w_g[:], xw[:].indirect(hc_t[:]))
        hc_w = tile([P, C], U32, "hc_w")
        nc.vector.tensor_copy(dealt(hc_w[:]), in_order(hc_w_g[:]))
        ca_w_g = tile([P, C], U32, "ca_w_g", tag=first_w1s)
        nc.vector.tensor_copy(ca_w_g[:], xw[:].indirect(ca_t[:]))
        ca_w = tile([P, C], U32, "ca_w")
        nc.vector.tensor_copy(dealt(ca_w[:]), in_order(ca_w_g[:]))
        ca_s_g = tile([P, C], U8, "ca_s_g", tag=first_hc_s)
        nc.vector.tensor_copy(ca_s_g[:], xs[:].indirect(ca_t[:]))
        ca_s = tile([P, C], U8, "ca_s")
        deal_bytes(ca_s, ca_s_g)

        a_ps = [ps.tile([P, S], F32, name=f"a_ps{t}", tag=f"bank{t}") for t in range(PACK)]

        def score_b(t, h):
            product(b_ps[t][:, HALVES[h]], t, hc_w, hc_s, z_w[h][:], z_s[h][:])
            nc.scalar.activation(b_sb[t][:, HALVES[h]], b_ps[t][:, HALVES[h]], COPY, scale=0.0625)

        def score_a(t, h):
            product(a_ps[t][:, HALVES[h]], t, ca_w, ca_s, z_w[h][:], z_s[h][:])

        minus_half_a = -0.5 * 0.0625
        for t in range(PACK):
            score_b(t, 0)
        for t in range(PACK):
            score_a(t, 0)
            nc.scalar.activation(a_sb[t][:, HALVES[0]], a_ps[t][:, HALVES[0]], COPY, scale=minus_half_a)
        for t in range(PACK):
            score_b(t, 1)
            score_a(t, 1)
            nc.vector.tensor_scalar_mul(a_sb[t][:, HALVES[1]], a_ps[t][:, HALVES[1]], minus_half_a)

        res_w = tile([P, S], U32, "res_w")
        res_s = tile([P, S], U8, "res_s")
        out_rows = out_0.rearrange("(p t) c -> p t c", t=PACK)
        out_words = out_1[0].rearrange("p n t -> p (n t)").bitcast(I32)
        fetched = tile([P, PACK, HALF], F32, "fetched")
        for h, cols in enumerate(HALVES):
            sg2 = tile([P, PACK, HALF], F32, f"sg2_{h}")
            gated = tile([P, PACK, HALF], F32, f"gated{h}")
            res = tile([P, PACK, HALF], F32, f"res{h}")
            fused = min(PACK, FETCHES_ON_VECTOR - PACK * h)
            for t in range(PACK):
                looked_up = a_sb[t][:].indirect(entries(n3_t, cols))
                if t >= fused:
                    nc.scalar.activation(fetched[:, t, :], looked_up, COPY)
                gate(sg2[:, t, :], b_sb[t], entries(n2_t, cols), t, sl2_t, bias2)
                nc.vector.scalar_tensor_tensor(gated[:, t, :], a_ps[t][:, cols], 0.0625, sg2[:, t, :], MULT, MULT)
                if t < fused:
                    nc.vector.tensor_tensor(res[:, t, :], looked_up, gated[:, t, :], ADD)
            if fused < PACK:
                for ts in (slice(fused, PACK - 1), slice(PACK - 1, PACK)):
                    nc.vector.tensor_tensor(res[:, ts, :], fetched[:, ts, :], gated[:, ts, :], ADD)
            nc.sync.dma_start(out_rows[:, :, cols], res[:])
            quantise(res, res_w[:, cols], res_s[:, cols], f"res_woven{h}")
            nc.sync.dma_start(out_words[:, cols], res_w[:, cols].bitcast(I32))
        for q in range(P // QUADRANT):
            queue = nc.scalar if q % 2 == 0 else nc.sync
            live = res_s[QUADRANT * q : QUADRANT * q + 4, :]
            queue.dma_start(out_2[0, 4 * q : 4 * q + 4, :].bitcast(I32), live.bitcast(I32))
